import numpy as np
import ml_dtypes


def mxq(x, axis, fmt="e4m3"):
    dtype, down = {"e4m3": (ml_dtypes.float8_e4m3fn, 7), "e5m2": (ml_dtypes.float8_e5m2, 14)}[fmt]
    v = np.moveaxis(np.asarray(x, np.float32).astype(ml_dtypes.bfloat16).astype(np.float64), axis, -1)
    blocks = v.reshape(v.shape[:-1] + (-1, 32))
    amax = np.abs(blocks).max(-1, keepdims=True)
    byte = np.maximum(np.where(amax > 0, np.frexp(amax)[1] - 1 + 127, 0) - down, 1)
    scale = np.exp2(byte - 127.0)
    codes = (blocks / scale).astype(np.float32).astype(dtype).astype(np.float64)
    return np.moveaxis((codes * scale).reshape(v.shape), -1, axis)


WIDE = False


def mx_kscale(k):
    if not WIDE:
        return np.ones(k)
    levels = np.array([10, -10, 5, -5, 0])
    if k % 512:
        return np.exp2(np.random.permutation(np.resize(levels, k // 32))).repeat(32)
    a = np.empty((k // 512, 16))
    for p in range(k // 512):
        a[p, :8] = np.random.permutation(np.resize(levels, 8))
        for g in range(8):
            far = levels[np.abs(levels - a[p, g]) >= 10]
            a[p, g + 8] = far[np.random.randint(len(far))]
    return np.exp2(a.ravel()).repeat(32)


def f64(x):
    return np.asarray(x).astype(np.float64)


def striped(idx):
    return np.tile(idx.reshape(-1, 16).T, (8, 1)).astype(np.uint16)


def unstriped(offs):
    return offs[:16].T.reshape(-1).astype(np.int64)


def striped8(idx):
    return np.concatenate([x.reshape(-1, 16).T for x in idx]).astype(np.uint16)


def runs(offs, k):
    lists = np.stack([offs[16 * r : 16 * r + 16].T.reshape(-1) for r in range(8)]).astype(np.int64)
    return lists[np.arange(k) % 512 // 64]


def pack_weight(w):
    k, n = w.shape
    w = f64(np.asarray(w, np.float32).astype(ml_dtypes.bfloat16)).reshape(k // 32, 32, n)
    amax = np.abs(w).max(1)
    byte = np.clip(np.where(amax > 0, np.frexp(amax)[1] - 1 + 127 - 7, 1), 1, 254)
    scaled = (w * np.exp2(127.0 - byte)[:, None, :]).reshape(k, n).astype(np.float32)
    words = np.ascontiguousarray(scaled.reshape(k // 512, 128, 4, n).transpose(0, 1, 3, 2)).astype(ml_dtypes.float8_e4m3fn).view(np.uint8)
    return words, np.ascontiguousarray(byte.astype(np.uint8).reshape(k // 512, 16, n))


def unpack_weight(words, scales):
    g, p, n, _ = words.shape
    vals = np.ascontiguousarray(words).view(ml_dtypes.float8_e4m3fn).astype(np.float64) * np.repeat(np.exp2(scales.astype(np.float64) - 127.0), 8, axis=1)[..., None]
    return vals.transpose(0, 1, 3, 2).reshape(g * 512, n)


K, T, S, N, H, W = 512, 2048, 256, 512, 512, 1024


def setup_inputs():
    n = np.random.standard_normal
    s = mx_kscale(K)[:, None]
    u = mx_kscale(H)
    packed_xT = pack_weight(n((K, T)) * s)
    return {
        "x_words": packed_xT[0],
        "x_scales": packed_xT[1],
        "w1": (n((K, H)) / np.sqrt(K) / s).astype(np.float32),
        "gn": (np.random.uniform(0.5, 1.5, (H, 1)) * u[:, None]).astype(np.float32),
        "w2": (n((H, N)) / np.sqrt(2 * H) / u[:, None]).astype(np.float32),
        "w3": (n((K, N)) / np.sqrt(2 * K) / s).astype(np.float32),
        "tau": np.random.uniform(0.3, 0.9, (N, 1)).astype(np.float32),
        "offs": striped(np.random.permutation(T)[:S]),
        "n1": striped(np.random.randint(0, S, W)),
        "two": striped(np.random.permutation(T)[:S]),
        "n2": striped8(np.stack([np.random.permutation(S) for _ in range(8)])),
        "n3": striped8(np.stack([np.random.permutation(S) for _ in range(8)])),
    }


def reference(x_words, x_scales, w1, gn, w2, w3, tau, offs, n1, two, n2, n3):
    xq = unpack_weight(x_words, x_scales)[:, unstriped(offs)]
    y = mxq(f64(w1), 0, "e4m3").T @ xq
    ex = np.exp(y)
    mb = ex[:, unstriped(n1)]
    ms = mb.reshape(H, S, 4).sum(axis=2)
    z = f64(gn) * (np.log(ms + ex) - y)
    x_two = unpack_weight(x_words, x_scales)[:, unstriped(two)]
    h = mxq(f64(w2), 0, "e4m3").T @ mxq(z, 0, "e4m3") + mxq(f64(w3), 0, "e4m3").T @ x_two
    top = h.max(axis=1, keepdims=True)
    ea = np.exp(f64(tau) * (h[np.arange(N)[:, None], runs(n2, N)] - top))
    return np.maximum(h, 2.0 * ea) - (0.5 * (h[np.arange(N)[:, None], runs(n3, N)]))

@@ -1,0 +1,252 @@
+from contextlib import ExitStack
+
+import concourse.mybir as mybir
+from concourse.masks import make_identity
+
+K, T, S, N, H, W = 512, 2048, 256, 512, 512, 1024
+FLOPS = 2 * K * H * S + 2 * H * N * S + 2 * K * N * S
+
+F32 = mybir.dt.float32
+BF16 = mybir.dt.bfloat16
+I32 = mybir.dt.int32
+U32 = mybir.dt.uint32
+U16 = mybir.dt.uint16
+U8 = mybir.dt.uint8
+FP8X4 = mybir.dt.float8_e4m3fn_x4
+ACT = mybir.ActivationFunctionType
+ALU = mybir.AluOpType
+
+P = 128
+PACK = 4
+MEMBERS = W // S
+HALF = S // 2
+EX_WINDOW = 1024
+H_WINDOW = 512
+VECTOR_PIECES = ((0, 0), (1, 0), (2, 0), (0, 1), (1, 1))
+
+
+def dealt(grouped, m0, m1):
+    return grouped.rearrange("p (t m j) -> p m t j", t=PACK, j=PACK)[:, m0:m1]
+
+
+def as_loaded(raw):
+    return raw.rearrange("p j (m t) -> p m t j", t=PACK)
+
+
+def tile_picked_mixinglseecl_none_p_kernel(
+    tc, x_words, x_scales, w1, gn, w2, w3, tau, offs, n1, two, n2, n3, out
+):
+    nc = tc.nc
+    with ExitStack() as ctx:
+        keep = ctx.enter_context(tc.tile_pool(name="keep", bufs=1))
+        psum = ctx.enter_context(tc.psum_pool(name="psum", bufs=1))
+
+        offs_sb = keep.tile([P, S // 16], U16, name="offs_sb")
+        two_sb = keep.tile([P, S // 16], U16, name="two_sb")
+        n1_sb = keep.tile([P, W // 16], U16, name="n1_sb")
+        n2_sb = keep.tile([P, S // 16], U16, name="n2_sb")
+        n3_sb = keep.tile([P, S // 16], U16, name="n3_sb")
+        words = keep.tile([P, T], I32, name="words", align_bytes=64)
+        scale_rows = keep.tile([P, T], U8, name="scale_rows", align_bytes=64)
+        w1_raw = [keep.tile([P, PACK, H // 2], F32, name=f"w1_raw{c}") for c in range(2)]
+        w2_raw = keep.tile([P, PACK, N], F32, name="w2_raw")
+        w3_raw = keep.tile([P, PACK, N], F32, name="w3_raw")
+        gn_sb = keep.tile([P, PACK], F32, name="gn_sb")
+        tau_sb = keep.tile([P, PACK], F32, name="tau_sb")
+
+        nc.vector.memset(scale_rows[:].bitcast(I32), 0)
+
+        w1_rows = w1.rearrange("(p j) c -> p j c", j=PACK)
+        nc.sync.dma_start(offs_sb[:], offs)
+        nc.sync.dma_start(w1_raw[0][:], w1_rows[:, :, : H // 2])
+        for q in range(4):
+            nc.sync.dma_start(
+                scale_rows[32 * q : 32 * q + 4, :].bitcast(I32),
+                x_scales[0, 4 * q : 4 * q + 4, :].bitcast(I32),
+            )
+        nc.sync.dma_start(w1_raw[1][:], w1_rows[:, :, H // 2 :])
+        nc.sync.dma_start(words[:], x_words[0].rearrange("p n t -> p (n t)").bitcast(I32))
+        nc.sync.dma_start(two_sb[:], two)
+        nc.sync.dma_start(n1_sb[:], n1)
+        nc.sync.dma_start(w3_raw[:], w3.rearrange("(p j) c -> p j c", j=PACK))
+        nc.sync.dma_start(w2_raw[:], w2.rearrange("(p j) c -> p j c", j=PACK))
+        nc.sync.dma_start(n2_sb[:], n2)
+        nc.sync.dma_start(n3_sb[:], n3)
+        nc.gpsimd.dma_start(tau_sb[:], tau.rearrange("(p t) o -> p (t o)", t=PACK))
+        nc.gpsimd.dma_start(gn_sb[:], gn.rearrange("(p t) o -> p (t o)", t=PACK))
+
+        ident = keep.tile([P, P], F32, name="ident")
+        make_identity(nc, ident[:])
+
+        ex = [keep.tile([P, EX_WINDOW], F32, name=f"ex{t}") for t in range(PACK)]
+        h = [keep.tile([P, H_WINDOW], F32, name=f"h{t}") for t in range(PACK)]
+        for t in range(PACK):
+            nc.vector.memset(ex[t][:, S:], 0.0)
+        for t in range(PACK):
+            nc.gpsimd.memset(h[t][:, S:], 0.0)
+
+        neg_tau = keep.tile([P, PACK], F32, name="neg_tau")
+        nc.scalar.activation(neg_tau[:], tau_sb[:], ACT.Copy, scale=-1.0)
+
+        w1_bf = keep.tile([P, PACK * H], BF16, name="w1_bf", align_bytes=64)
+        nc.scalar.copy(dealt(w1_bf[:], 0, P // 2), as_loaded(w1_raw[0][:]))
+        nc.vector.tensor_copy(dealt(w1_bf[:], P // 2, P), as_loaded(w1_raw[1][:]))
+        w1_codes = keep.tile([P, H], U32, name="w1_codes", align_bytes=64)
+        w1_scales = keep.tile([P, H], U8, name="w1_scales", align_bytes=64)
+        nc.vector.quantize_mx(w1_codes[:].bitcast(FP8X4), w1_scales[:], w1_bf[:])
+
+        xq_codes = keep.tile([P, S], U32, name="xq_codes", align_bytes=64)
+        xq_scales = keep.tile([P, S], U8, name="xq_scales", align_bytes=64)
+        xt_codes = keep.tile([P, S], U32, name="xt_codes", align_bytes=64)
+        xt_scales = keep.tile([P, S], U8, name="xt_scales", align_bytes=64)
+        nc.vector.tensor_copy(xq_scales[:], scale_rows[:].indirect(offs_sb[:]))
+        nc.vector.tensor_copy(xq_codes[:], words[:].bitcast(U32).indirect(offs_sb[:]))
+        nc.vector.tensor_copy(xt_scales[:], scale_rows[:].indirect(two_sb[:]))
+        nc.vector.tensor_copy(xt_codes[:], words[:].bitcast(U32).indirect(two_sb[:]))
+
+        y = []
+        for t in range(PACK):
+            y_t = psum.tile([P, S], F32, name=f"y{t}", tag=f"bank{t}")
+            cols = slice(P * t, P * (t + 1))
+            nc.tensor.matmul_mx(
+                y_t[:],
+                lhsT=w1_codes[:, cols].bitcast(FP8X4),
+                lhsT_scale=w1_scales[:, cols],
+                rhs=xq_codes[:].bitcast(FP8X4),
+                rhs_scale=xq_scales[:],
+                start=True,
+                stop=True,
+            )
+            nc.scalar.activation(ex[t][:, :S], y_t[:], ACT.Exp)
+            y.append(y_t)
+
+        sums = {}
+        for half in range(2):
+            entries = n1_sb[:, 32 * half : 32 * (half + 1)]
+            for pair in range(2):
+                bank = psum.tile([P, 2, P], F32, name=f"sum{half}{pair}", tag=f"bank{4 + 2 * half + pair}")
+                sums[half, pair] = bank
+                for slot in range(2):
+                    t = 2 * pair + slot
+                    if (t, half) in VECTOR_PIECES:
+                        mb = keep.tile([P, MEMBERS, HALF], F32, name=f"mb{t}{half}")
+                        nc.vector.tensor_copy(mb[:].rearrange("p u j -> p j u"), ex[t][:].indirect(entries))
+                        terms = [mb[:, u, :] for u in range(MEMBERS)]
+                    else:
+                        mb = keep.tile([P, HALF * MEMBERS], F32, name=f"mb{t}{half}")
+                        nc.scalar.activation(mb[:], ex[t][:].indirect(entries), ACT.Copy)
+                        terms = [mb[:, u::MEMBERS] for u in range(MEMBERS)]
+                    terms = [ex[t][:, HALF * half : HALF * (half + 1)]] + terms
+                    for u in range(len(terms)):
+                        nc.tensor.matmul(
+                            bank[:, slot, :],
+                            lhsT=terms[u],
+                            rhs=ident[:],
+                            is_transpose=True,
+                            start=(u == 0),
+                            stop=(u == len(terms) - 1),
+                        )
+
+        w23_bf = keep.tile([P, 2, PACK * N], BF16, name="w23_bf", align_bytes=64)
+        for a, raw in enumerate((w3_raw, w2_raw)):
+            for m0 in (0, P // 2):
+                nc.gpsimd.tensor_scalar(
+                    dealt(w23_bf[:, a, :], m0, m0 + P // 2),
+                    as_loaded(raw[:])[:, m0 : m0 + P // 2],
+                    1.0,
+                    0.0,
+                    ALU.mult,
+                    ALU.add,
+                )
+        w23_codes = keep.tile([P, 2 * N], U32, name="w23_codes", align_bytes=64)
+        w23_scales = keep.tile([P, 2 * N], U8, name="w23_scales", align_bytes=64)
+        nc.vector.quantize_mx(
+            w23_codes[:].bitcast(FP8X4), w23_scales[:], w23_bf[:].rearrange("p a c -> p (a c)")
+        )
+
+        def log_and_turn_back(half):
+            backs = []
+            for pair in range(2):
+                log_t = keep.tile([P, 2, P], F32, name=f"log_t{half}{pair}")
+                nc.scalar.activation(log_t[:], sums[half, pair][:], ACT.Ln)
+                back = psum.tile([P, 2, HALF], F32, name=f"back{half}{pair}", tag=f"bank{4 + 2 * half + pair}")
+                for slot in range(2):
+                    nc.tensor.transpose(back[:, slot, :], log_t[:, slot, :], ident[:])
+                backs.append(back)
+            return backs
+
+        def quantise_z(half, backs):
+            js = slice(HALF * half, HALF * (half + 1))
+            z_rows = keep.tile([P, PACK, HALF], BF16, name=f"z_rows{half}")
+            for t in range(PACK):
+                nc.vector.scalar_tensor_tensor(
+                    z_rows[:, t, :],
+                    backs[t // 2][:, t % 2, :],
+                    gn_sb[:, t : t + 1],
+                    yg[t][:, js],
+                    ALU.mult,
+                    ALU.subtract,
+                )
+            z_bf = keep.tile([P, HALF * PACK], BF16, name=f"z_bf{half}", align_bytes=64)
+            nc.vector.tensor_copy(
+                z_bf[:].rearrange("p (c i t) -> p c t i", i=4, t=PACK),
+                z_rows[:].rearrange("p t (c i) -> p c t i", i=4),
+            )
+            z_codes = keep.tile([P, HALF], U32, name=f"z_codes{half}", align_bytes=64)
+            z_scales = keep.tile([P, HALF], U8, name=f"z_scales{half}", align_bytes=64)
+            nc.vector.quantize_mx(z_codes[:].bitcast(FP8X4), z_scales[:], z_bf[:])
+            return z_codes, z_scales
+
+        backs0 = log_and_turn_back(0)
+        yg = []
+        for t in range(PACK):
+            yg_t = keep.tile([P, S], F32, name=f"yg{t}")
+            nc.scalar.activation(yg_t[:], y[t][:], ACT.Copy, scale=gn_sb[:, t : t + 1])
+            yg.append(yg_t)
+        backs1 = log_and_turn_back(1)
+
+        acc = [psum.tile([P, S], F32, name=f"acc{t}", tag=f"bank{t}") for t in range(PACK)]
+        for t in range(PACK):
+            cols = slice(P * t, P * (t + 1))
+            nc.tensor.matmul_mx(
+                acc[t][:],
+                lhsT=w23_codes[:, cols].bitcast(FP8X4),
+                lhsT_scale=w23_scales[:, cols],
+                rhs=xt_codes[:].bitcast(FP8X4),
+                rhs_scale=xt_scales[:],
+                start=True,
+                stop=False,
+            )
+        for half, backs in enumerate((backs0, backs1)):
+            z_codes, z_scales = quantise_z(half, backs)
+            for t in range(PACK):
+                cols = slice(N + P * t, N + P * (t + 1))
+                nc.tensor.matmul_mx(
+                    acc[t][:, HALF * half : HALF * (half + 1)],
+                    lhsT=w23_codes[:, cols].bitcast(FP8X4),
+                    lhsT_scale=w23_scales[:, cols],
+                    rhs=z_codes[:].bitcast(FP8X4),
+                    rhs_scale=z_scales[:],
+                    start=False,
+                    stop=(half == 1),
+                )
+
+        out_rows = out.rearrange("(p t) j -> p t j", t=PACK)
+        for t in range(PACK):
+            top = keep.tile([P, 1], F32, name=f"top{t}")
+            nc.vector.tensor_scalar(
+                h[t][:, :S], acc[t][:], 1.0, None, ALU.mult, ALU.max, accum_out=top[:]
+            )
+            bias = keep.tile([P, 1], F32, name=f"bias{t}")
+            nc.vector.tensor_tensor(bias[:], top[:], neg_tau[:, t : t + 1], ALU.mult)
+            ea = keep.tile([P, S], F32, name=f"ea{t}")
+            nc.scalar.activation(
+                ea[:], h[t][:].indirect(n2_sb[:]), ACT.Exp, bias=bias[:], scale=tau_sb[:, t : t + 1]
+            )
+            h3 = keep.tile([P, S], F32, name=f"h3{t}")
+            nc.scalar.activation(h3[:], h[t][:].indirect(n3_sb[:]), ACT.Copy)
+            larger = keep.tile([P, S], F32, name=f"larger{t}")
+            nc.vector.scalar_tensor_tensor(larger[:], ea[:], 2.0, h[t][:, :S], ALU.mult, ALU.max)
+            res = keep.tile([P, S], F32, name=f"res{t}")
+            nc.vector.scalar_tensor_tensor(res[:], h3[:], -0.5, larger[:], ALU.mult, ALU.add)
+            nc.sync.dma_start(out_rows[:, t, :], res[:])

@@ -22,7 +22,7 @@ MEMBERS = W // S
 HALF = S // 2
 EX_WINDOW = 1024
 H_WINDOW = 512
-VECTOR_PIECES = ((0, 0), (1, 0), (2, 0), (0, 1), (1, 1))
+VECTOR_PIECES = ((0, 0), (1, 0), (0, 1), (1, 1))
 
 
 def dealt(grouped, m0, m1):
@@ -68,12 +68,12 @@ def tile_picked_mixinglseecl_none_p_kernel(
         nc.sync.dma_start(words[:], x_words[0].rearrange("p n t -> p (n t)").bitcast(I32))
         nc.sync.dma_start(two_sb[:], two)
         nc.sync.dma_start(n1_sb[:], n1)
+        nc.sync.dma_start(gn_sb[:], gn.rearrange("(p t) o -> p (t o)", t=PACK))
         nc.sync.dma_start(w3_raw[:], w3.rearrange("(p j) c -> p j c", j=PACK))
         nc.sync.dma_start(w2_raw[:], w2.rearrange("(p j) c -> p j c", j=PACK))
         nc.sync.dma_start(n2_sb[:], n2)
         nc.sync.dma_start(n3_sb[:], n3)
-        nc.gpsimd.dma_start(tau_sb[:], tau.rearrange("(p t) o -> p (t o)", t=PACK))
-        nc.gpsimd.dma_start(gn_sb[:], gn.rearrange("(p t) o -> p (t o)", t=PACK))
+        nc.scalar.dma_start(tau_sb[:], tau.rearrange("(p t) o -> p (t o)", t=PACK))
 
         ident = keep.tile([P, P], F32, name="ident")
         make_identity(nc, ident[:])
@@ -83,7 +83,7 @@ def tile_picked_mixinglseecl_none_p_kernel(
         for t in range(PACK):
             nc.vector.memset(ex[t][:, S:], 0.0)
         for t in range(PACK):
-            nc.gpsimd.memset(h[t][:, S:], 0.0)
+            nc.vector.memset(h[t][:, S:], 0.0)
 
         neg_tau = keep.tile([P, PACK], F32, name="neg_tau")
         nc.scalar.activation(neg_tau[:], tau_sb[:], ACT.Copy, scale=-1.0)
@@ -149,15 +149,7 @@ def tile_picked_mixinglseecl_none_p_kernel(
 
         w23_bf = keep.tile([P, 2, PACK * N], BF16, name="w23_bf", align_bytes=64)
         for a, raw in enumerate((w3_raw, w2_raw)):
-            for m0 in (0, P // 2):
-                nc.gpsimd.tensor_scalar(
-                    dealt(w23_bf[:, a, :], m0, m0 + P // 2),
-                    as_loaded(raw[:])[:, m0 : m0 + P // 2],
-                    1.0,
-                    0.0,
-                    ALU.mult,
-                    ALU.add,
-                )
+            nc.vector.tensor_copy(dealt(w23_bf[:, a, :], 0, P), as_loaded(raw[:]))
         w23_codes = keep.tile([P, 2 * N], U32, name="w23_codes", align_bytes=64)
         w23_scales = keep.tile([P, 2 * N], U8, name="w23_scales", align_bytes=64)
         nc.vector.quantize_mx(
@@ -197,12 +189,12 @@ def tile_picked_mixinglseecl_none_p_kernel(
             nc.vector.quantize_mx(z_codes[:].bitcast(FP8X4), z_scales[:], z_bf[:])
             return z_codes, z_scales
 
+        yg = [keep.tile([P, S], F32, name=f"yg{t}") for t in range(PACK)]
+        for t in range(2):
+            nc.vector.tensor_scalar(yg[t][:], y[t][:], gn_sb[:, t : t + 1], None, ALU.mult)
         backs0 = log_and_turn_back(0)
-        yg = []
-        for t in range(PACK):
-            yg_t = keep.tile([P, S], F32, name=f"yg{t}")
-            nc.scalar.activation(yg_t[:], y[t][:], ACT.Copy, scale=gn_sb[:, t : t + 1])
-            yg.append(yg_t)
+        for t in range(2, PACK):
+            nc.scalar.activation(yg[t][:], y[t][:], ACT.Copy, scale=gn_sb[:, t : t + 1])
         backs1 = log_and_turn_back(1)
 
         acc = [psum.tile([P, S], F32, name=f"acc{t}", tag=f"bank{t}") for t in range(PACK)]
@@ -240,11 +232,14 @@ def tile_picked_mixinglseecl_none_p_kernel(
             bias = keep.tile([P, 1], F32, name=f"bias{t}")
             nc.vector.tensor_tensor(bias[:], top[:], neg_tau[:, t : t + 1], ALU.mult)
             ea = keep.tile([P, S], F32, name=f"ea{t}")
+            h3 = keep.tile([P, S], F32, name=f"h3{t}")
+            if t == 0:
+                nc.scalar.activation(h3[:], h[t][:].indirect(n3_sb[:]), ACT.Copy)
             nc.scalar.activation(
                 ea[:], h[t][:].indirect(n2_sb[:]), ACT.Exp, bias=bias[:], scale=tau_sb[:, t : t + 1]
             )
-            h3 = keep.tile([P, S], F32, name=f"h3{t}")
-            nc.scalar.activation(h3[:], h[t][:].indirect(n3_sb[:]), ACT.Copy)
+            if t > 0:
+                nc.scalar.activation(h3[:], h[t][:].indirect(n3_sb[:]), ACT.Copy)
             larger = keep.tile([P, S], F32, name=f"larger{t}")
             nc.vector.scalar_tensor_tensor(larger[:], ea[:], 2.0, h[t][:, :S], ALU.mult, ALU.max)
             res = keep.tile([P, S], F32, name=f"res{t}")

@@ -22,6 +22,7 @@ MEMBERS = W // S
 HALF = S // 2
 EX_WINDOW = 1024
 H_WINDOW = 512
+W2_SPLIT = 64
 VECTOR_PIECES = ((0, 0), (1, 0), (0, 1), (1, 1))
 
 
@@ -133,9 +134,15 @@ def tile_picked_mixinglseecl_none_p_kernel(
                         nc.vector.tensor_copy(mb[:].rearrange("p u j -> p j u"), ex[t][:].indirect(entries))
                         terms = [mb[:, u, :] for u in range(MEMBERS)]
                     else:
-                        mb = keep.tile([P, HALF * MEMBERS], F32, name=f"mb{t}{half}")
-                        nc.scalar.activation(mb[:], ex[t][:].indirect(entries), ACT.Copy)
-                        terms = [mb[:, u::MEMBERS] for u in range(MEMBERS)]
+                        mb = keep.tile([P, HALF, MEMBERS], F32, name=f"mb{t}{half}")
+                        nc.scalar.activation(
+                            mb[:].rearrange("p j u -> p (j u)"), ex[t][:].indirect(entries), ACT.Copy
+                        )
+                        pairs = keep.tile([P, 2, HALF], F32, name=f"pairs{t}{half}")
+                        nc.vector.tensor_tensor(
+                            pairs[:].rearrange("p u j -> p j u"), mb[:, :, 0:2], mb[:, :, 2:4], ALU.add
+                        )
+                        terms = [pairs[:, u, :] for u in range(2)]
                     terms = [ex[t][:, HALF * half : HALF * (half + 1)]] + terms
                     for u in range(len(terms)):
                         nc.tensor.matmul(
@@ -147,14 +154,15 @@ def tile_picked_mixinglseecl_none_p_kernel(
                             stop=(u == len(terms) - 1),
                         )
 
-        w23_bf = keep.tile([P, 2, PACK * N], BF16, name="w23_bf", align_bytes=64)
-        for a, raw in enumerate((w3_raw, w2_raw)):
-            nc.vector.tensor_copy(dealt(w23_bf[:, a, :], 0, P), as_loaded(raw[:]))
-        w23_codes = keep.tile([P, 2 * N], U32, name="w23_codes", align_bytes=64)
-        w23_scales = keep.tile([P, 2 * N], U8, name="w23_scales", align_bytes=64)
-        nc.vector.quantize_mx(
-            w23_codes[:].bitcast(FP8X4), w23_scales[:], w23_bf[:].rearrange("p a c -> p (a c)")
-        )
+        w3_bf = keep.tile([P, PACK * N], BF16, name="w3_bf", align_bytes=64)
+        w2_bf = keep.tile([P, PACK * N], BF16, name="w2_bf", align_bytes=64)
+        w3_codes = keep.tile([P, N], U32, name="w3_codes", align_bytes=64)
+        w3_scales = keep.tile([P, N], U8, name="w3_scales", align_bytes=64)
+        w2_codes = keep.tile([P, N], U32, name="w2_codes", align_bytes=64)
+        w2_scales = keep.tile([P, N], U8, name="w2_scales", align_bytes=64)
+        nc.vector.tensor_copy(dealt(w3_bf[:], 0, P), as_loaded(w3_raw[:]))
+        nc.vector.tensor_copy(dealt(w2_bf[:], 0, W2_SPLIT), as_loaded(w2_raw[:])[:, :W2_SPLIT])
+        nc.vector.quantize_mx(w3_codes[:].bitcast(FP8X4), w3_scales[:], w3_bf[:])
 
         def log_and_turn_back(half):
             backs = []
@@ -167,7 +175,7 @@ def tile_picked_mixinglseecl_none_p_kernel(
                 backs.append(back)
             return backs
 
-        def quantise_z(half, backs):
+        def round_z(half, backs):
             js = slice(HALF * half, HALF * (half + 1))
             z_rows = keep.tile([P, PACK, HALF], BF16, name=f"z_rows{half}")
             for t in range(PACK):
@@ -184,39 +192,44 @@ def tile_picked_mixinglseecl_none_p_kernel(
                 z_bf[:].rearrange("p (c i t) -> p c t i", i=4, t=PACK),
                 z_rows[:].rearrange("p t (c i) -> p c t i", i=4),
             )
+            return z_bf
+
+        def quantise_z(half, z_bf):
             z_codes = keep.tile([P, HALF], U32, name=f"z_codes{half}", align_bytes=64)
             z_scales = keep.tile([P, HALF], U8, name=f"z_scales{half}", align_bytes=64)
             nc.vector.quantize_mx(z_codes[:].bitcast(FP8X4), z_scales[:], z_bf[:])
             return z_codes, z_scales
 
         yg = [keep.tile([P, S], F32, name=f"yg{t}") for t in range(PACK)]
-        for t in range(2):
-            nc.vector.tensor_scalar(yg[t][:], y[t][:], gn_sb[:, t : t + 1], None, ALU.mult)
         backs0 = log_and_turn_back(0)
-        for t in range(2, PACK):
+        for t in range(PACK):
             nc.scalar.activation(yg[t][:], y[t][:], ACT.Copy, scale=gn_sb[:, t : t + 1])
         backs1 = log_and_turn_back(1)
+        nc.scalar.copy(dealt(w2_bf[:], W2_SPLIT, P), as_loaded(w2_raw[:])[:, W2_SPLIT:])
 
         acc = [psum.tile([P, S], F32, name=f"acc{t}", tag=f"bank{t}") for t in range(PACK)]
         for t in range(PACK):
             cols = slice(P * t, P * (t + 1))
             nc.tensor.matmul_mx(
                 acc[t][:],
-                lhsT=w23_codes[:, cols].bitcast(FP8X4),
-                lhsT_scale=w23_scales[:, cols],
+                lhsT=w3_codes[:, cols].bitcast(FP8X4),
+                lhsT_scale=w3_scales[:, cols],
                 rhs=xt_codes[:].bitcast(FP8X4),
                 rhs_scale=xt_scales[:],
                 start=True,
                 stop=False,
             )
-        for half, backs in enumerate((backs0, backs1)):
-            z_codes, z_scales = quantise_z(half, backs)
+        z = [quantise_z(0, round_z(0, backs0))]
+        z_bf1 = round_z(1, backs1)
+        nc.vector.quantize_mx(w2_codes[:].bitcast(FP8X4), w2_scales[:], w2_bf[:])
+        z.append(quantise_z(1, z_bf1))
+        for half, (z_codes, z_scales) in enumerate(z):
             for t in range(PACK):
-                cols = slice(N + P * t, N + P * (t + 1))
+                cols = slice(P * t, P * (t + 1))
                 nc.tensor.matmul_mx(
                     acc[t][:, HALF * half : HALF * (half + 1)],
-                    lhsT=w23_codes[:, cols].bitcast(FP8X4),
-                    lhsT_scale=w23_scales[:, cols],
+                    lhsT=w2_codes[:, cols].bitcast(FP8X4),
+                    lhsT_scale=w2_scales[:, cols],
                     rhs=z_codes[:].bitcast(FP8X4),
                     rhs_scale=z_scales[:],
                     start=False,

@@ -18,16 +18,17 @@ ALU = mybir.AluOpType
 
 P = 128
 PACK = 4
+GROUP = 16
 MEMBERS = W // S
 HALF = S // 2
-EX_WINDOW = 1024
-H_WINDOW = 512
-W2_SPLIT = 64
-VECTOR_PIECES = ((0, 0), (1, 0), (0, 1), (1, 1))
+EX_WINDOW = 2 * MEMBERS * HALF
+H_WINDOW = 2 * S
+TILES_ON_VECTOR = 2
+YG_ON_VECTOR = 3
 
 
 def dealt(grouped, m0, m1):
-    return grouped.rearrange("p (t m j) -> p m t j", t=PACK, j=PACK)[:, m0:m1]
+    return grouped.rearrange("p (t m j) -> p m t j", m=P, j=PACK)[:, m0:m1]
 
 
 def as_loaded(raw):
@@ -42,11 +43,11 @@ def tile_picked_mixinglseecl_none_p_kernel(
         keep = ctx.enter_context(tc.tile_pool(name="keep", bufs=1))
         psum = ctx.enter_context(tc.psum_pool(name="psum", bufs=1))
 
-        offs_sb = keep.tile([P, S // 16], U16, name="offs_sb")
-        two_sb = keep.tile([P, S // 16], U16, name="two_sb")
-        n1_sb = keep.tile([P, W // 16], U16, name="n1_sb")
-        n2_sb = keep.tile([P, S // 16], U16, name="n2_sb")
-        n3_sb = keep.tile([P, S // 16], U16, name="n3_sb")
+        offs_sb = keep.tile([P, S // GROUP], U16, name="offs_sb")
+        two_sb = keep.tile([P, S // GROUP], U16, name="two_sb")
+        n1_sb = keep.tile([P, W // GROUP], U16, name="n1_sb")
+        n2_sb = keep.tile([P, S // GROUP], U16, name="n2_sb")
+        n3_sb = keep.tile([P, S // GROUP], U16, name="n3_sb")
         words = keep.tile([P, T], I32, name="words", align_bytes=64)
         scale_rows = keep.tile([P, T], U8, name="scale_rows", align_bytes=64)
         w1_raw = [keep.tile([P, PACK, H // 2], F32, name=f"w1_raw{c}") for c in range(2)]
@@ -122,27 +123,22 @@ def tile_picked_mixinglseecl_none_p_kernel(
             y.append(y_t)
 
         sums = {}
+        columns_a_piece = MEMBERS * HALF // GROUP
         for half in range(2):
-            entries = n1_sb[:, 32 * half : 32 * (half + 1)]
+            entries = n1_sb[:, columns_a_piece * half : columns_a_piece * (half + 1)]
             for pair in range(2):
                 bank = psum.tile([P, 2, P], F32, name=f"sum{half}{pair}", tag=f"bank{4 + 2 * half + pair}")
                 sums[half, pair] = bank
                 for slot in range(2):
                     t = 2 * pair + slot
-                    if (t, half) in VECTOR_PIECES:
+                    if t < TILES_ON_VECTOR:
                         mb = keep.tile([P, MEMBERS, HALF], F32, name=f"mb{t}{half}")
                         nc.vector.tensor_copy(mb[:].rearrange("p u j -> p j u"), ex[t][:].indirect(entries))
                         terms = [mb[:, u, :] for u in range(MEMBERS)]
                     else:
-                        mb = keep.tile([P, HALF, MEMBERS], F32, name=f"mb{t}{half}")
-                        nc.scalar.activation(
-                            mb[:].rearrange("p j u -> p (j u)"), ex[t][:].indirect(entries), ACT.Copy
-                        )
-                        pairs = keep.tile([P, 2, HALF], F32, name=f"pairs{t}{half}")
-                        nc.vector.tensor_tensor(
-                            pairs[:].rearrange("p u j -> p j u"), mb[:, :, 0:2], mb[:, :, 2:4], ALU.add
-                        )
-                        terms = [pairs[:, u, :] for u in range(2)]
+                        mb = keep.tile([P, HALF * MEMBERS], F32, name=f"mb{t}{half}")
+                        nc.scalar.activation(mb[:], ex[t][:].indirect(entries), ACT.Copy)
+                        terms = [mb[:, u::MEMBERS] for u in range(MEMBERS)]
                     terms = [ex[t][:, HALF * half : HALF * (half + 1)]] + terms
                     for u in range(len(terms)):
                         nc.tensor.matmul(
@@ -155,57 +151,40 @@ def tile_picked_mixinglseecl_none_p_kernel(
                         )
 
         w3_bf = keep.tile([P, PACK * N], BF16, name="w3_bf", align_bytes=64)
-        w2_bf = keep.tile([P, PACK * N], BF16, name="w2_bf", align_bytes=64)
+        w2_bf = keep.tile([P, 2 * PACK * P], BF16, name="w2_bf", align_bytes=64)
         w3_codes = keep.tile([P, N], U32, name="w3_codes", align_bytes=64)
         w3_scales = keep.tile([P, N], U8, name="w3_scales", align_bytes=64)
-        w2_codes = keep.tile([P, N], U32, name="w2_codes", align_bytes=64)
-        w2_scales = keep.tile([P, N], U8, name="w2_scales", align_bytes=64)
+        w2_codes = keep.tile([P, N // 2], U32, name="w2_codes", align_bytes=64)
+        w2_scales = keep.tile([P, N // 2], U8, name="w2_scales", align_bytes=64)
         nc.vector.tensor_copy(dealt(w3_bf[:], 0, P), as_loaded(w3_raw[:]))
-        nc.vector.tensor_copy(dealt(w2_bf[:], 0, W2_SPLIT), as_loaded(w2_raw[:])[:, :W2_SPLIT])
+        nc.vector.tensor_copy(dealt(w2_bf[:], 0, P), as_loaded(w2_raw[:])[:, :, 0:2])
         nc.vector.quantize_mx(w3_codes[:].bitcast(FP8X4), w3_scales[:], w3_bf[:])
+        nc.vector.quantize_mx(w2_codes[:].bitcast(FP8X4), w2_scales[:], w2_bf[:])
 
-        def log_and_turn_back(half):
-            backs = []
-            for pair in range(2):
-                log_t = keep.tile([P, 2, P], F32, name=f"log_t{half}{pair}")
-                nc.scalar.activation(log_t[:], sums[half, pair][:], ACT.Ln)
-                back = psum.tile([P, 2, HALF], F32, name=f"back{half}{pair}", tag=f"bank{4 + 2 * half + pair}")
-                for slot in range(2):
-                    nc.tensor.transpose(back[:, slot, :], log_t[:, slot, :], ident[:])
-                backs.append(back)
-            return backs
+        back = {}
 
-        def round_z(half, backs):
-            js = slice(HALF * half, HALF * (half + 1))
-            z_rows = keep.tile([P, PACK, HALF], BF16, name=f"z_rows{half}")
-            for t in range(PACK):
-                nc.vector.scalar_tensor_tensor(
-                    z_rows[:, t, :],
-                    backs[t // 2][:, t % 2, :],
-                    gn_sb[:, t : t + 1],
-                    yg[t][:, js],
-                    ALU.mult,
-                    ALU.subtract,
-                )
-            z_bf = keep.tile([P, HALF * PACK], BF16, name=f"z_bf{half}", align_bytes=64)
-            nc.vector.tensor_copy(
-                z_bf[:].rearrange("p (c i t) -> p c t i", i=4, t=PACK),
-                z_rows[:].rearrange("p t (c i) -> p c t i", i=4),
-            )
-            return z_bf
-
-        def quantise_z(half, z_bf):
-            z_codes = keep.tile([P, HALF], U32, name=f"z_codes{half}", align_bytes=64)
-            z_scales = keep.tile([P, HALF], U8, name=f"z_scales{half}", align_bytes=64)
-            nc.vector.quantize_mx(z_codes[:].bitcast(FP8X4), z_scales[:], z_bf[:])
-            return z_codes, z_scales
+        def log_and_turn_back(half, pair):
+            log_t = keep.tile([P, 2, P], F32, name=f"log_t{half}{pair}", tag=f"log_t{half}{pair}", align_bytes=64)
+            nc.scalar.activation(log_t[:], sums[half, pair][:], ACT.Ln)
+            bank = psum.tile([P, 2, HALF], F32, name=f"back{half}{pair}", tag=f"bank{4 + 2 * half + pair}")
+            for slot in range(2):
+                nc.tensor.transpose(bank[:, slot, :], log_t[:, slot, :], ident[:])
+                back[2 * pair + slot, half] = bank[:, slot, :]
 
         yg = [keep.tile([P, S], F32, name=f"yg{t}") for t in range(PACK)]
-        backs0 = log_and_turn_back(0)
-        for t in range(PACK):
+        for t in range(YG_ON_VECTOR):
+            nc.vector.tensor_scalar(yg[t][:], y[t][:], gn_sb[:, t : t + 1], None, ALU.mult)
+        log_and_turn_back(0, 0)
+        log_and_turn_back(0, 1)
+        log_and_turn_back(1, 0)
+        for t in range(YG_ON_VECTOR, PACK):
             nc.scalar.activation(yg[t][:], y[t][:], ACT.Copy, scale=gn_sb[:, t : t + 1])
-        backs1 = log_and_turn_back(1)
-        nc.scalar.copy(dealt(w2_bf[:], W2_SPLIT, P), as_loaded(w2_raw[:])[:, W2_SPLIT:])
+        log_and_turn_back(1, 1)
+
+        w2_late = keep.tile([P, 2 * PACK * P], BF16, name="w2_late", tag="log_t10", align_bytes=64)
+        nc.scalar.copy(dealt(w2_late[:], 0, P), as_loaded(w2_raw[:])[:, :, 2:4])
+        exp_warm_up = keep.tile([P, 1], F32, name="exp_warm_up")
+        nc.scalar.activation(exp_warm_up[:], w2_late[:, 0:1], ACT.Exp, scale=0.0)
 
         acc = [psum.tile([P, S], F32, name=f"acc{t}", tag=f"bank{t}") for t in range(PACK)]
         for t in range(PACK):
@@ -219,22 +198,42 @@ def tile_picked_mixinglseecl_none_p_kernel(
                 start=True,
                 stop=False,
             )
-        z = [quantise_z(0, round_z(0, backs0))]
-        z_bf1 = round_z(1, backs1)
-        nc.vector.quantize_mx(w2_codes[:].bitcast(FP8X4), w2_scales[:], w2_bf[:])
-        z.append(quantise_z(1, z_bf1))
-        for half, (z_codes, z_scales) in enumerate(z):
+
+        z_codes = keep.tile([P, S], U32, name="z_codes", align_bytes=64)
+        z_scales = keep.tile([P, S], U8, name="z_scales", align_bytes=64)
+
+        def times_w2(t, js, codes, scales):
+            cols = slice(P * (t % 2), P * (t % 2 + 1))
+            nc.tensor.matmul_mx(
+                acc[t][:, js],
+                lhsT=codes[:, cols].bitcast(FP8X4),
+                lhsT_scale=scales[:, cols],
+                rhs=z_codes[:, js].bitcast(FP8X4),
+                rhs_scale=z_scales[:, js],
+                start=False,
+                stop=(js.stop == S),
+            )
+
+        for half in range(2):
+            js = slice(HALF * half, HALF * (half + 1))
+            z_rows = keep.tile([P, PACK, HALF], BF16, name=f"z_rows{half}")
             for t in range(PACK):
-                cols = slice(P * t, P * (t + 1))
-                nc.tensor.matmul_mx(
-                    acc[t][:, HALF * half : HALF * (half + 1)],
-                    lhsT=w2_codes[:, cols].bitcast(FP8X4),
-                    lhsT_scale=w2_scales[:, cols],
-                    rhs=z_codes[:].bitcast(FP8X4),
-                    rhs_scale=z_scales[:],
-                    start=False,
-                    stop=(half == 1),
+                nc.vector.scalar_tensor_tensor(
+                    z_rows[:, t, :], back[t, half], gn_sb[:, t : t + 1], yg[t][:, js], ALU.mult, ALU.subtract
                 )
+            z_bf = keep.tile([P, HALF * PACK], BF16, name=f"z_bf{half}", tag=f"z_bf{half}", align_bytes=64)
+            nc.vector.tensor_copy(
+                z_bf[:].rearrange("p (c i t) -> p c t i", i=4, t=PACK),
+                z_rows[:].rearrange("p t (c i) -> p c t i", i=4),
+            )
+            nc.vector.quantize_mx(z_codes[:, js].bitcast(FP8X4), z_scales[:, js], z_bf[:])
+            for t in range(2):
+                times_w2(t, js, w2_codes, w2_scales)
+        late_codes = keep.tile([P, N // 2], U32, name="late_codes", tag="z_bf1", align_bytes=64)
+        late_scales = keep.tile([P, N // 2], U8, name="late_scales", align_bytes=64)
+        nc.vector.quantize_mx(late_codes[:].bitcast(FP8X4), late_scales[:], w2_late[:])
+        for t in range(2, PACK):
+            times_w2(t, slice(0, S), late_codes, late_scales)
 
         out_rows = out.rearrange("(p t) j -> p t j", t=PACK)
         for t in range(PACK):
@@ -251,10 +250,15 @@ def tile_picked_mixinglseecl_none_p_kernel(
             nc.scalar.activation(
                 ea[:], h[t][:].indirect(n2_sb[:]), ACT.Exp, bias=bias[:], scale=tau_sb[:, t : t + 1]
             )
-            if t > 0:
-                nc.scalar.activation(h3[:], h[t][:].indirect(n3_sb[:]), ACT.Copy)
             larger = keep.tile([P, S], F32, name=f"larger{t}")
             nc.vector.scalar_tensor_tensor(larger[:], ea[:], 2.0, h[t][:, :S], ALU.mult, ALU.max)
-            res = keep.tile([P, S], F32, name=f"res{t}")
-            nc.vector.scalar_tensor_tensor(res[:], h3[:], -0.5, larger[:], ALU.mult, ALU.add)
-            nc.sync.dma_start(out_rows[:, t, :], res[:])
+            parts = 2 if t == PACK - 1 else 1
+            width = S // parts
+            for part in range(parts):
+                js = slice(width * part, width * (part + 1))
+                if t > 0:
+                    places = n3_sb[:, js.start // GROUP : js.stop // GROUP]
+                    nc.scalar.activation(h3[:, js], h[t][:].indirect(places), ACT.Copy)
+                res = keep.tile([P, width], F32, name=f"res{t}{part}")
+                nc.vector.scalar_tensor_tensor(res[:], h3[:, js], -0.5, larger[:, js], ALU.mult, ALU.add)
+                nc.sync.dma_start(out_rows[:, t, js], res[:])

from contextlib import ExitStack

import concourse.mybir as mybir
from concourse.masks import make_identity

K, T, S, N, H, W = 512, 2048, 256, 512, 512, 1024
FLOPS = 2 * K * H * S + 2 * H * N * S + 2 * K * N * S

F32 = mybir.dt.float32
BF16 = mybir.dt.bfloat16
I32 = mybir.dt.int32
U32 = mybir.dt.uint32
U16 = mybir.dt.uint16
U8 = mybir.dt.uint8
FP8X4 = mybir.dt.float8_e4m3fn_x4
ACT = mybir.ActivationFunctionType
ALU = mybir.AluOpType

P = 128
PACK = 4
GROUP = 16
MEMBERS = W // S
HALF = S // 2
EX_WINDOW = 2 * MEMBERS * HALF
H_WINDOW = 2 * S
TILES_ON_VECTOR = 2
YG_ON_VECTOR = 3


def dealt(grouped, m0, m1):
    return grouped.rearrange("p (t m j) -> p m t j", m=P, j=PACK)[:, m0:m1]


def as_loaded(raw):
    return raw.rearrange("p j (m t) -> p m t j", t=PACK)


def tile_picked_mixinglseecl_none_p_kernel(
    tc, x_words, x_scales, w1, gn, w2, w3, tau, offs, n1, two, n2, n3, out
):
    nc = tc.nc
    with ExitStack() as ctx:
        keep = ctx.enter_context(tc.tile_pool(name="keep", bufs=1))
        psum = ctx.enter_context(tc.psum_pool(name="psum", bufs=1))

        offs_sb = keep.tile([P, S // GROUP], U16, name="offs_sb")
        two_sb = keep.tile([P, S // GROUP], U16, name="two_sb")
        n1_sb = keep.tile([P, W // GROUP], U16, name="n1_sb")
        n2_sb = keep.tile([P, S // GROUP], U16, name="n2_sb")
        n3_sb = keep.tile([P, S // GROUP], U16, name="n3_sb")
        words = keep.tile([P, T], I32, name="words", align_bytes=64)
        scale_rows = keep.tile([P, T], U8, name="scale_rows", align_bytes=64)
        w1_raw = [keep.tile([P, PACK, H // 2], F32, name=f"w1_raw{c}") for c in range(2)]
        w2_raw = keep.tile([P, PACK, N], F32, name="w2_raw")
        w3_raw = keep.tile([P, PACK, N], F32, name="w3_raw")
        gn_sb = keep.tile([P, PACK], F32, name="gn_sb")
        tau_sb = keep.tile([P, PACK], F32, name="tau_sb")

        nc.vector.memset(scale_rows[:].bitcast(I32), 0)

        w1_rows = w1.rearrange("(p j) c -> p j c", j=PACK)
        nc.sync.dma_start(offs_sb[:], offs)
        nc.sync.dma_start(w1_raw[0][:], w1_rows[:, :, : H // 2])
        for q in range(4):
            nc.sync.dma_start(
                scale_rows[32 * q : 32 * q + 4, :].bitcast(I32),
                x_scales[0, 4 * q : 4 * q + 4, :].bitcast(I32),
            )
        nc.sync.dma_start(w1_raw[1][:], w1_rows[:, :, H // 2 :])
        nc.sync.dma_start(words[:], x_words[0].rearrange("p n t -> p (n t)").bitcast(I32))
        nc.sync.dma_start(two_sb[:], two)
        nc.sync.dma_start(n1_sb[:], n1)
        nc.sync.dma_start(gn_sb[:], gn.rearrange("(p t) o -> p (t o)", t=PACK))
        nc.sync.dma_start(w3_raw[:], w3.rearrange("(p j) c -> p j c", j=PACK))
        nc.sync.dma_start(w2_raw[:], w2.rearrange("(p j) c -> p j c", j=PACK))
        nc.sync.dma_start(n2_sb[:], n2)
        nc.sync.dma_start(n3_sb[:], n3)
        nc.scalar.dma_start(tau_sb[:], tau.rearrange("(p t) o -> p (t o)", t=PACK))

        ident = keep.tile([P, P], F32, name="ident")
        make_identity(nc, ident[:])

        ex = [keep.tile([P, EX_WINDOW], F32, name=f"ex{t}") for t in range(PACK)]
        h = [keep.tile([P, H_WINDOW], F32, name=f"h{t}") for t in range(PACK)]
        for t in range(PACK):
            nc.vector.memset(ex[t][:, S:], 0.0)
        for t in range(PACK):
            nc.vector.memset(h[t][:, S:], 0.0)

        neg_tau = keep.tile([P, PACK], F32, name="neg_tau")
        nc.scalar.activation(neg_tau[:], tau_sb[:], ACT.Copy, scale=-1.0)

        w1_bf = keep.tile([P, PACK * H], BF16, name="w1_bf", align_bytes=64)
        nc.scalar.copy(dealt(w1_bf[:], 0, P // 2), as_loaded(w1_raw[0][:]))
        nc.vector.tensor_copy(dealt(w1_bf[:], P // 2, P), as_loaded(w1_raw[1][:]))
        w1_codes = keep.tile([P, H], U32, name="w1_codes", align_bytes=64)
        w1_scales = keep.tile([P, H], U8, name="w1_scales", align_bytes=64)
        nc.vector.quantize_mx(w1_codes[:].bitcast(FP8X4), w1_scales[:], w1_bf[:])

        xq_codes = keep.tile([P, S], U32, name="xq_codes", align_bytes=64)
        xq_scales = keep.tile([P, S], U8, name="xq_scales", align_bytes=64)
        xt_codes = keep.tile([P, S], U32, name="xt_codes", align_bytes=64)
        xt_scales = keep.tile([P, S], U8, name="xt_scales", align_bytes=64)
        nc.vector.tensor_copy(xq_scales[:], scale_rows[:].indirect(offs_sb[:]))
        nc.vector.tensor_copy(xq_codes[:], words[:].bitcast(U32).indirect(offs_sb[:]))
        nc.vector.tensor_copy(xt_scales[:], scale_rows[:].indirect(two_sb[:]))
        nc.vector.tensor_copy(xt_codes[:], words[:].bitcast(U32).indirect(two_sb[:]))

        y = []
        for t in range(PACK):
            y_t = psum.tile([P, S], F32, name=f"y{t}", tag=f"bank{t}")
            cols = slice(P * t, P * (t + 1))
            nc.tensor.matmul_mx(
                y_t[:],
                lhsT=w1_codes[:, cols].bitcast(FP8X4),
                lhsT_scale=w1_scales[:, cols],
                rhs=xq_codes[:].bitcast(FP8X4),
                rhs_scale=xq_scales[:],
                start=True,
                stop=True,
            )
            nc.scalar.activation(ex[t][:, :S], y_t[:], ACT.Exp)
            y.append(y_t)

        sums = {}
        columns_a_piece = MEMBERS * HALF // GROUP
        for half in range(2):
            entries = n1_sb[:, columns_a_piece * half : columns_a_piece * (half + 1)]
            for pair in range(2):
                bank = psum.tile([P, 2, P], F32, name=f"sum{half}{pair}", tag=f"bank{4 + 2 * half + pair}")
                sums[half, pair] = bank
                for slot in range(2):
                    t = 2 * pair + slot
                    if t < TILES_ON_VECTOR:
                        mb = keep.tile([P, MEMBERS, HALF], F32, name=f"mb{t}{half}")
                        nc.vector.tensor_copy(mb[:].rearrange("p u j -> p j u"), ex[t][:].indirect(entries))
                        terms = [mb[:, u, :] for u in range(MEMBERS)]
                    else:
                        mb = keep.tile([P, HALF * MEMBERS], F32, name=f"mb{t}{half}")
                        nc.scalar.activation(mb[:], ex[t][:].indirect(entries), ACT.Copy)
                        terms = [mb[:, u::MEMBERS] for u in range(MEMBERS)]
                    terms = [ex[t][:, HALF * half : HALF * (half + 1)]] + terms
                    for u in range(len(terms)):
                        nc.tensor.matmul(
                            bank[:, slot, :],
                            lhsT=terms[u],
                            rhs=ident[:],
                            is_transpose=True,
                            start=(u == 0),
                            stop=(u == len(terms) - 1),
                        )

        w3_bf = keep.tile([P, PACK * N], BF16, name="w3_bf", align_bytes=64)
        w2_bf = keep.tile([P, 2 * PACK * P], BF16, name="w2_bf", align_bytes=64)
        w3_codes = keep.tile([P, N], U32, name="w3_codes", align_bytes=64)
        w3_scales = keep.tile([P, N], U8, name="w3_scales", align_bytes=64)
        w2_codes = keep.tile([P, N // 2], U32, name="w2_codes", align_bytes=64)
        w2_scales = keep.tile([P, N // 2], U8, name="w2_scales", align_bytes=64)
        nc.vector.tensor_copy(dealt(w3_bf[:], 0, P), as_loaded(w3_raw[:]))
        nc.vector.tensor_copy(dealt(w2_bf[:], 0, P), as_loaded(w2_raw[:])[:, :, 0:2])
        nc.vector.quantize_mx(w3_codes[:].bitcast(FP8X4), w3_scales[:], w3_bf[:])
        nc.vector.quantize_mx(w2_codes[:].bitcast(FP8X4), w2_scales[:], w2_bf[:])

        back = {}

        def log_and_turn_back(half, pair):
            log_t = keep.tile([P, 2, P], F32, name=f"log_t{half}{pair}", tag=f"log_t{half}{pair}", align_bytes=64)
            nc.scalar.activation(log_t[:], sums[half, pair][:], ACT.Ln)
            bank = psum.tile([P, 2, HALF], F32, name=f"back{half}{pair}", tag=f"bank{4 + 2 * half + pair}")
            for slot in range(2):
                nc.tensor.transpose(bank[:, slot, :], log_t[:, slot, :], ident[:])
                back[2 * pair + slot, half] = bank[:, slot, :]

        yg = [keep.tile([P, S], F32, name=f"yg{t}") for t in range(PACK)]
        for t in range(YG_ON_VECTOR):
            nc.vector.tensor_scalar(yg[t][:], y[t][:], gn_sb[:, t : t + 1], None, ALU.mult)
        log_and_turn_back(0, 0)
        log_and_turn_back(0, 1)
        log_and_turn_back(1, 0)
        for t in range(YG_ON_VECTOR, PACK):
            nc.scalar.activation(yg[t][:], y[t][:], ACT.Copy, scale=gn_sb[:, t : t + 1])
        log_and_turn_back(1, 1)

        w2_late = keep.tile([P, 2 * PACK * P], BF16, name="w2_late", tag="log_t10", align_bytes=64)
        nc.scalar.copy(dealt(w2_late[:], 0, P), as_loaded(w2_raw[:])[:, :, 2:4])
        exp_warm_up = keep.tile([P, 1], F32, name="exp_warm_up")
        nc.scalar.activation(exp_warm_up[:], w2_late[:, 0:1], ACT.Exp, scale=0.0)

        acc = [psum.tile([P, S], F32, name=f"acc{t}", tag=f"bank{t}") for t in range(PACK)]
        for t in range(PACK):
            cols = slice(P * t, P * (t + 1))
            nc.tensor.matmul_mx(
                acc[t][:],
                lhsT=w3_codes[:, cols].bitcast(FP8X4),
                lhsT_scale=w3_scales[:, cols],
                rhs=xt_codes[:].bitcast(FP8X4),
                rhs_scale=xt_scales[:],
                start=True,
                stop=False,
            )

        z_codes = keep.tile([P, S], U32, name="z_codes", align_bytes=64)
        z_scales = keep.tile([P, S], U8, name="z_scales", align_bytes=64)

        def times_w2(t, js, codes, scales):
            cols = slice(P * (t % 2), P * (t % 2 + 1))
            nc.tensor.matmul_mx(
                acc[t][:, js],
                lhsT=codes[:, cols].bitcast(FP8X4),
                lhsT_scale=scales[:, cols],
                rhs=z_codes[:, js].bitcast(FP8X4),
                rhs_scale=z_scales[:, js],
                start=False,
                stop=(js.stop == S),
            )

        for half in range(2):
            js = slice(HALF * half, HALF * (half + 1))
            z_rows = keep.tile([P, PACK, HALF], BF16, name=f"z_rows{half}")
            for t in range(PACK):
                nc.vector.scalar_tensor_tensor(
                    z_rows[:, t, :], back[t, half], gn_sb[:, t : t + 1], yg[t][:, js], ALU.mult, ALU.subtract
                )
            z_bf = keep.tile([P, HALF * PACK], BF16, name=f"z_bf{half}", tag=f"z_bf{half}", align_bytes=64)
            nc.vector.tensor_copy(
                z_bf[:].rearrange("p (c i t) -> p c t i", i=4, t=PACK),
                z_rows[:].rearrange("p t (c i) -> p c t i", i=4),
            )
            nc.vector.quantize_mx(z_codes[:, js].bitcast(FP8X4), z_scales[:, js], z_bf[:])
            for t in range(2):
                times_w2(t, js, w2_codes, w2_scales)
        late_codes = keep.tile([P, N // 2], U32, name="late_codes", tag="z_bf1", align_bytes=64)
        late_scales = keep.tile([P, N // 2], U8, name="late_scales", align_bytes=64)
        nc.vector.quantize_mx(late_codes[:].bitcast(FP8X4), late_scales[:], w2_late[:])
        for t in range(2, PACK):
            times_w2(t, slice(0, S), late_codes, late_scales)

        out_rows = out.rearrange("(p t) j -> p t j", t=PACK)
        for t in range(PACK):
            top = keep.tile([P, 1], F32, name=f"top{t}")
            nc.vector.tensor_scalar(
                h[t][:, :S], acc[t][:], 1.0, None, ALU.mult, ALU.max, accum_out=top[:]
            )
            bias = keep.tile([P, 1], F32, name=f"bias{t}")
            nc.vector.tensor_tensor(bias[:], top[:], neg_tau[:, t : t + 1], ALU.mult)
            ea = keep.tile([P, S], F32, name=f"ea{t}")
            h3 = keep.tile([P, S], F32, name=f"h3{t}")
            if t == 0:
                nc.scalar.activation(h3[:], h[t][:].indirect(n3_sb[:]), ACT.Copy)
            nc.scalar.activation(
                ea[:], h[t][:].indirect(n2_sb[:]), ACT.Exp, bias=bias[:], scale=tau_sb[:, t : t + 1]
            )
            larger = keep.tile([P, S], F32, name=f"larger{t}")
            nc.vector.scalar_tensor_tensor(larger[:], ea[:], 2.0, h[t][:, :S], ALU.mult, ALU.max)
            parts = 2 if t == PACK - 1 else 1
            width = S // parts
            for part in range(parts):
                js = slice(width * part, width * (part + 1))
                if t > 0:
                    places = n3_sb[:, js.start // GROUP : js.stop // GROUP]
                    nc.scalar.activation(h3[:, js], h[t][:].indirect(places), ACT.Copy)
                res = keep.tile([P, width], F32, name=f"res{t}{part}")
                nc.vector.scalar_tensor_tensor(res[:], h3[:, js], -0.5, larger[:, js], ALU.mult, ALU.add)
                nc.sync.dma_start(out_rows[:, t, js], res[:])
